import numpy as np
import ml_dtypes


def mxq(x, axis, fmt="e4m3"):
    dtype, down = {"e4m3": (ml_dtypes.float8_e4m3fn, 7), "e5m2": (ml_dtypes.float8_e5m2, 14)}[fmt]
    v = np.moveaxis(np.asarray(x, np.float32).astype(ml_dtypes.bfloat16).astype(np.float64), axis, -1)
    blocks = v.reshape(v.shape[:-1] + (-1, 32))
    amax = np.abs(blocks).max(-1, keepdims=True)
    byte = np.maximum(np.where(amax > 0, np.frexp(amax)[1] - 1 + 127, 0) - down, 1)
    scale = np.exp2(byte - 127.0)
    codes = (blocks / scale).astype(np.float32).astype(dtype).astype(np.float64)
    return np.moveaxis((codes * scale).reshape(v.shape), -1, axis)


WIDE = False


def mx_kscale(k):
    if not WIDE:
        return np.ones(k)
    levels = np.array([10, -10, 5, -5, 0])
    if k % 512:
        return np.exp2(np.random.permutation(np.resize(levels, k // 32))).repeat(32)
    a = np.empty((k // 512, 16))
    for p in range(k // 512):
        a[p, :8] = np.random.permutation(np.resize(levels, 8))
        for g in range(8):
            far = levels[np.abs(levels - a[p, g]) >= 10]
            a[p, g + 8] = far[np.random.randint(len(far))]
    return np.exp2(a.ravel()).repeat(32)


def f64(x):
    return np.asarray(x).astype(np.float64)


def striped(idx):
    return np.tile(idx.reshape(-1, 16).T, (8, 1)).astype(np.uint16)


def unstriped(offs):
    return offs[:16].T.reshape(-1).astype(np.int64)


def pack_weight(w):
    k, n = w.shape
    w = f64(np.asarray(w, np.float32).astype(ml_dtypes.bfloat16)).reshape(k // 32, 32, n)
    amax = np.abs(w).max(1)
    byte = np.clip(np.where(amax > 0, np.frexp(amax)[1] - 1 + 127 - 7, 1), 1, 254)
    scaled = (w * np.exp2(127.0 - byte)[:, None, :]).reshape(k, n).astype(np.float32)
    words = np.ascontiguousarray(scaled.reshape(k // 512, 128, 4, n).transpose(0, 1, 3, 2)).astype(ml_dtypes.float8_e4m3fn).view(np.uint8)
    return words, np.ascontiguousarray(byte.astype(np.uint8).reshape(k // 512, 16, n))


def unpack_weight(words, scales):
    g, p, n, _ = words.shape
    vals = np.ascontiguousarray(words).view(ml_dtypes.float8_e4m3fn).astype(np.float64) * np.repeat(np.exp2(scales.astype(np.float64) - 127.0), 8, axis=1)[..., None]
    return vals.transpose(0, 1, 3, 2).reshape(g * 512, n)


def relu(v):
    return np.maximum(v, 0.0)


K, T, S, V, N = 1024, 2048, 512, 256, 128


def setup_inputs():
    n = np.random.standard_normal
    s = mx_kscale(K)[:, None]
    packed_w1 = pack_weight(n((K, N)) / np.sqrt(K) / s)
    packed_w2 = pack_weight(n((K, N)) / np.sqrt(K) / s)
    packed_w3 = pack_weight(n((K, N)) / np.sqrt(K) / s)
    return {
        "xT": (n((K, T)) * s).astype(np.float32),
        "w1_words": packed_w1[0],
        "w1_scales": packed_w1[1],
        "w2_words": packed_w2[0],
        "w2_scales": packed_w2[1],
        "w3_words": packed_w3[0],
        "w3_scales": packed_w3[1],
        "offs": striped(np.random.permutation(T)[:S]),
        "cen": striped(np.random.permutation(S)[:V]),
        "pos1": striped(np.random.permutation(S)[:V]),
        "pos2": striped(np.random.permutation(S)[:V]),
    }


def reference(xT, w1_words, w1_scales, w2_words, w2_scales, w3_words, w3_scales, offs, cen, pos1, pos2):
    xq = mxq(f64(xT)[:, unstriped(offs)], 0, "e4m3")
    h = unpack_weight(w3_words, w3_scales).T @ xq
    g = unpack_weight(w1_words, w1_scales).T @ xq
    gc = g[:, unstriped(cen)]
    s = unpack_weight(w2_words, w2_scales).T @ xq
    sc = s[:, unstriped(cen)]
    return relu(h[:, unstriped(pos1)] * gc + sc) + relu(h[:, unstriped(pos2)] * gc + sc)

@@ -1,0 +1,131 @@
+from contextlib import ExitStack
+
+import concourse.mybir as mybir
+
+K, T, S, V, N = 1024, 2048, 512, 256, 128
+FLOPS = 3 * 2 * K * S * N
+
+F32 = mybir.dt.float32
+BF16 = mybir.dt.bfloat16
+I32 = mybir.dt.int32
+U32 = mybir.dt.uint32
+U16 = mybir.dt.uint16
+U8 = mybir.dt.uint8
+FP8X4 = mybir.dt.float8_e4m3fn_x4
+ALU = mybir.AluOpType
+ACT = mybir.ActivationFunctionType
+
+P = 128
+PACK = 4
+K_PASS = P * PACK
+PASSES = K // K_PASS
+HALVES = 2
+S_HALF = S // HALVES
+LIST_COL = 16
+QUADS = 4
+ROWS = 4
+
+
+def tile_picked_filmg_relu_e_kernel(
+    tc, xT, w1_words, w1_scales, w2_words, w2_scales, w3_words, w3_scales, offs, cen, pos1, pos2, out
+):
+    nc = tc.nc
+    words_in = [w1_words, w2_words, w3_words]
+    scales_in = [w1_scales, w2_scales, w3_scales]
+    n_w = len(words_in)
+
+    with ExitStack() as ctx:
+        keep = ctx.enter_context(tc.tile_pool(name="keep", bufs=1))
+        psum = ctx.enter_context(tc.psum_pool(name="psum", bufs=1))
+
+        offs_t = keep.tile([P, S // LIST_COL], U16, name="offs_t")
+        cen_t = keep.tile([P, V // LIST_COL], U16, name="cen_t")
+        pos1_t = keep.tile([P, V // LIST_COL], U16, name="pos1_t")
+        pos2_t = keep.tile([P, V // LIST_COL], U16, name="pos2_t")
+
+        planes = [keep.tile([P, T], F32, name=f"plane{i}") for i in range(PASSES * PACK)]
+        x_rows = xT.rearrange("(z p j) t -> z j p t", z=PASSES, j=PACK)
+
+        staged = keep.tile([QUADS * ROWS, n_w, PASSES, N], U8, name="staged")
+        w_scale = keep.tile([P, n_w, PASSES, N], U8, name="w_scale", align_bytes=64)
+        w_code = [keep.tile([P, PASSES, N], U32, name=f"w_code{w}", align_bytes=64) for w in range(n_w)]
+
+        nc.gpsimd.memset(w_scale[:].rearrange("p w z n -> p (w z n)").bitcast(I32), 0)
+
+        nc.sync.dma_start(planes[0][:], x_rows[0, 0])
+        nc.sync.dma_start(offs_t[:], offs)
+        for w in range(n_w):
+            nc.sync.dma_start(
+                staged[:, w].bitcast(I32), scales_in[w].rearrange("z s n -> s z n").bitcast(I32)
+            )
+        for i in range(1, PASSES * PACK):
+            nc.sync.dma_start(planes[i][:], x_rows[i // PACK, i % PACK])
+        for q in range(QUADS):
+            nc.sync.dma_start(
+                w_scale[32 * q : 32 * q + ROWS].rearrange("p w z n -> p (w z n)").bitcast(I32),
+                staged[ROWS * q : ROWS * (q + 1)].rearrange("p w z n -> p (w z n)").bitcast(I32),
+            )
+        for w in range(n_w):
+            nc.sync.dma_start(
+                w_code[w][:].bitcast(I32), words_in[w].rearrange("z p n t -> p z (n t)").bitcast(I32)
+            )
+        nc.sync.dma_start(cen_t[:], cen)
+        nc.sync.dma_start(pos1_t[:], pos1)
+        nc.sync.dma_start(pos2_t[:], pos2)
+
+        x_code = {}
+        x_scale = {}
+        for z in range(PASSES):
+            picked = [keep.tile([P, S_HALF, PACK], BF16, name=f"picked{z}{h}", align_bytes=64) for h in range(HALVES)]
+            for j in range(PACK):
+                for h in range(HALVES):
+                    cols = slice(h * S_HALF // LIST_COL, (h + 1) * S_HALF // LIST_COL)
+                    nc.vector.tensor_copy(picked[h][:, :, j], planes[z * PACK + j][:].indirect(offs_t[:, cols]))
+            for h in range(HALVES):
+                x_code[z, h] = keep.tile([P, S_HALF], U32, name=f"x_code{z}{h}", align_bytes=64)
+                x_scale[z, h] = keep.tile([P, S_HALF], U8, name=f"x_scale{z}{h}", align_bytes=64)
+                nc.vector.quantize_mx(
+                    out=x_code[z, h][:].bitcast(FP8X4),
+                    scales=x_scale[z, h][:],
+                    in_=picked[h][:].rearrange("p s j -> p (s j)"),
+                )
+
+        acc = {}
+        for w in range(n_w):
+            for h in range(HALVES):
+                acc[w, h] = psum.tile([P, S_HALF], F32, name=f"acc{w}{h}")
+        for z in range(PASSES):
+            for w in range(n_w):
+                for h in range(HALVES):
+                    nc.tensor.matmul_mx(
+                        out=acc[w, h][:],
+                        lhsT=w_code[w][:, z, :].bitcast(FP8X4),
+                        lhsT_scale=w_scale[:, w, z, :],
+                        rhs=x_code[z, h][:].bitcast(FP8X4),
+                        rhs_scale=x_scale[z, h][:],
+                        start=(z == 0),
+                        stop=(z == PASSES - 1),
+                    )
+        res = [keep.tile([P, S], F32, name=f"res{w}") for w in range(n_w)]
+        for w in range(n_w):
+            for h in range(HALVES):
+                nc.scalar.copy(res[w][:, h * S_HALF : (h + 1) * S_HALF], acc[w, h][:])
+        g, s, hh = res
+
+        gc = keep.tile([P, V], F32, name="gc")
+        sc = keep.tile([P, V], F32, name="sc")
+        t1 = keep.tile([P, V], F32, name="t1")
+        t2 = keep.tile([P, V], F32, name="t2")
+        a1 = keep.tile([P, V], F32, name="a1")
+        a2 = keep.tile([P, V], F32, name="a2")
+        r1 = keep.tile([P, V], F32, name="r1")
+        y = keep.tile([P, V], F32, name="y")
+        nc.vector.tensor_copy(gc[:], g[:].indirect(cen_t[:]))
+        nc.vector.tensor_copy(sc[:], s[:].indirect(cen_t[:]))
+        nc.vector.tensor_tensor(t1[:], hh[:].indirect(pos1_t[:]), gc[:], ALU.mult)
+        nc.vector.tensor_tensor(t2[:], hh[:].indirect(pos2_t[:]), gc[:], ALU.mult)
+        nc.vector.tensor_tensor(a1[:], t1[:], sc[:], ALU.add)
+        nc.vector.tensor_tensor(a2[:], t2[:], sc[:], ALU.add)
+        nc.scalar.activation(r1[:], a1[:], ACT.Relu)
+        nc.vector.scalar_tensor_tensor(y[:], a2[:], 0.0, r1[:], ALU.max, ALU.add)
+        nc.sync.dma_start(out, y[:])

@@ -48,7 +48,11 @@ def tile_picked_filmg_relu_e_kernel(
 
         staged = keep.tile([QUADS * ROWS, n_w, PASSES, N], U8, name="staged")
         w_scale = keep.tile([P, n_w, PASSES, N], U8, name="w_scale", align_bytes=64)
-        w_code = [keep.tile([P, PASSES, N], U32, name=f"w_code{w}", align_bytes=64) for w in range(n_w)]
+        w_code = {
+            (w, z): keep.tile([P, N], U32, name=f"w_code{w}{z}", align_bytes=64)
+            for w in range(n_w)
+            for z in range(PASSES)
+        }
 
         nc.gpsimd.memset(w_scale[:].rearrange("p w z n -> p (w z n)").bitcast(I32), 0)
 
@@ -61,14 +65,15 @@ def tile_picked_filmg_relu_e_kernel(
         for i in range(1, PASSES * PACK):
             nc.sync.dma_start(planes[i][:], x_rows[i // PACK, i % PACK])
         for q in range(QUADS):
-            nc.sync.dma_start(
+            nc.gpsimd.dma_start(
                 w_scale[32 * q : 32 * q + ROWS].rearrange("p w z n -> p (w z n)").bitcast(I32),
                 staged[ROWS * q : ROWS * (q + 1)].rearrange("p w z n -> p (w z n)").bitcast(I32),
             )
-        for w in range(n_w):
-            nc.sync.dma_start(
-                w_code[w][:].bitcast(I32), words_in[w].rearrange("z p n t -> p z (n t)").bitcast(I32)
-            )
+        for z in range(PASSES):
+            for w in range(n_w):
+                nc.sync.dma_start(
+                    w_code[w, z][:].bitcast(I32), words_in[w][z].rearrange("p n t -> p (n t)").bitcast(I32)
+                )
         nc.sync.dma_start(cen_t[:], cen)
         nc.sync.dma_start(pos1_t[:], pos1)
         nc.sync.dma_start(pos2_t[:], pos2)
@@ -99,7 +104,7 @@ def tile_picked_filmg_relu_e_kernel(
                 for h in range(HALVES):
                     nc.tensor.matmul_mx(
                         out=acc[w, h][:],
-                        lhsT=w_code[w][:, z, :].bitcast(FP8X4),
+                        lhsT=w_code[w, z][:].bitcast(FP8X4),
                         lhsT_scale=w_scale[:, w, z, :],
                         rhs=x_code[z, h][:].bitcast(FP8X4),
                         rhs_scale=x_scale[z, h][:],

@@ -24,6 +24,7 @@ S_HALF = S // HALVES
 LIST_COL = 16
 QUADS = 4
 ROWS = 4
+GROUPS = [[(0, 256), (256, 384), (384, 512)], [(0, 256), (256, 512)], [(0, 256), (256, 512)]]
 
 
 def tile_picked_filmg_relu_e_kernel(
@@ -43,8 +44,10 @@ def tile_picked_filmg_relu_e_kernel(
         pos1_t = keep.tile([P, V // LIST_COL], U16, name="pos1_t")
         pos2_t = keep.tile([P, V // LIST_COL], U16, name="pos2_t")
 
-        planes = [keep.tile([P, T], F32, name=f"plane{i}") for i in range(PASSES * PACK)]
-        x_rows = xT.rearrange("(z p j) t -> z j p t", z=PASSES, j=PACK)
+        groups = [(0, 0, 2), (0, 2, 2), (1, 0, 2), (1, 2, 1), (1, 3, 1)]
+        loaded = [keep.tile([P, n, T], F32, name=f"planes{z}{j}") for z, j, n in groups]
+        plane = {(z, j + i): loaded[g][:, i, :] for g, (z, j, n) in enumerate(groups) for i in range(n)}
+        x_rows = xT.rearrange("(z p j) t -> z p j t", z=PASSES, j=PACK)
 
         staged = keep.tile([QUADS * ROWS, n_w, PASSES, N], U8, name="staged")
         w_scale = keep.tile([P, n_w, PASSES, N], U8, name="w_scale", align_bytes=64)
@@ -54,67 +57,76 @@ def tile_picked_filmg_relu_e_kernel(
             for z in range(PASSES)
         }
 
-        nc.gpsimd.memset(w_scale[:].rearrange("p w z n -> p (w z n)").bitcast(I32), 0)
+        scale_words = w_scale[:].rearrange("p w z n -> p (w z n)").bitcast(I32)
+        staged_words = staged[:].rearrange("p w z n -> p (w z n)").bitcast(I32)
+        nc.gpsimd.memset(scale_words, 0)
 
-        nc.sync.dma_start(planes[0][:], x_rows[0, 0])
-        nc.sync.dma_start(offs_t[:], offs)
         for w in range(n_w):
-            nc.sync.dma_start(
+            nc.scalar.dma_start(
                 staged[:, w].bitcast(I32), scales_in[w].rearrange("z s n -> s z n").bitcast(I32)
             )
-        for i in range(1, PASSES * PACK):
-            nc.sync.dma_start(planes[i][:], x_rows[i // PACK, i % PACK])
+        for g, (z, j, n) in enumerate(groups):
+            nc.sync.dma_start(loaded[g][:], x_rows[z, :, j : j + n, :])
+            if g == 0:
+                nc.sync.dma_start(offs_t[:], offs)
         for q in range(QUADS):
-            nc.gpsimd.dma_start(
-                w_scale[32 * q : 32 * q + ROWS].rearrange("p w z n -> p (w z n)").bitcast(I32),
-                staged[ROWS * q : ROWS * (q + 1)].rearrange("p w z n -> p (w z n)").bitcast(I32),
-            )
+            nc.gpsimd.dma_start(scale_words[32 * q : 32 * q + ROWS], staged_words[ROWS * q : ROWS * (q + 1)])
         for z in range(PASSES):
             for w in range(n_w):
                 nc.sync.dma_start(
                     w_code[w, z][:].bitcast(I32), words_in[w][z].rearrange("p n t -> p (n t)").bitcast(I32)
                 )
-        nc.sync.dma_start(cen_t[:], cen)
-        nc.sync.dma_start(pos1_t[:], pos1)
         nc.sync.dma_start(pos2_t[:], pos2)
+        nc.sync.dma_start(pos1_t[:], pos1)
+        nc.sync.dma_start(cen_t[:], cen)
 
         x_code = {}
         x_scale = {}
         for z in range(PASSES):
             picked = [keep.tile([P, S_HALF, PACK], BF16, name=f"picked{z}{h}", align_bytes=64) for h in range(HALVES)]
-            for j in range(PACK):
+            first = 0
+            if z == PASSES - 1:
+                first = 2
                 for h in range(HALVES):
                     cols = slice(h * S_HALF // LIST_COL, (h + 1) * S_HALF // LIST_COL)
-                    nc.vector.tensor_copy(picked[h][:, :, j], planes[z * PACK + j][:].indirect(offs_t[:, cols]))
-            for h in range(HALVES):
-                x_code[z, h] = keep.tile([P, S_HALF], U32, name=f"x_code{z}{h}", align_bytes=64)
-                x_scale[z, h] = keep.tile([P, S_HALF], U8, name=f"x_scale{z}{h}", align_bytes=64)
+                    pair = keep.tile([P, 2, S_HALF], F32, name=f"pair{h}")
+                    for j in range(first):
+                        nc.vector.tensor_copy(pair[:, j, :], plane[z, j].indirect(offs_t[:, cols]))
+                    nc.scalar.copy(picked[h][:, :, :first], pair[:].rearrange("p j s -> p s j"))
+            for j in range(first, PACK):
+                for h in range(HALVES):
+                    cols = slice(h * S_HALF // LIST_COL, (h + 1) * S_HALF // LIST_COL)
+                    nc.vector.tensor_copy(picked[h][:, :, j], plane[z, j].indirect(offs_t[:, cols]))
+            x_code[z] = keep.tile([P, S], U32, name=f"x_code{z}", align_bytes=64)
+            x_scale[z] = keep.tile([P, S], U8, name=f"x_scale{z}", align_bytes=64)
+            for lo, hi in GROUPS[0]:
+                h = lo // S_HALF
                 nc.vector.quantize_mx(
-                    out=x_code[z, h][:].bitcast(FP8X4),
-                    scales=x_scale[z, h][:],
-                    in_=picked[h][:].rearrange("p s j -> p (s j)"),
+                    out=x_code[z][:, lo:hi].bitcast(FP8X4),
+                    scales=x_scale[z][:, lo:hi],
+                    in_=picked[h][:, lo - h * S_HALF : hi - h * S_HALF].rearrange("p s j -> p (s j)"),
                 )
 
         acc = {}
         for w in range(n_w):
-            for h in range(HALVES):
-                acc[w, h] = psum.tile([P, S_HALF], F32, name=f"acc{w}{h}")
+            for lo, hi in GROUPS[w]:
+                acc[w, lo] = psum.tile([P, hi - lo], F32, name=f"acc{w}_{lo}")
         for z in range(PASSES):
             for w in range(n_w):
-                for h in range(HALVES):
+                for lo, hi in GROUPS[w]:
                     nc.tensor.matmul_mx(
-                        out=acc[w, h][:],
+                        out=acc[w, lo][:],
                         lhsT=w_code[w, z][:].bitcast(FP8X4),
                         lhsT_scale=w_scale[:, w, z, :],
-                        rhs=x_code[z, h][:].bitcast(FP8X4),
-                        rhs_scale=x_scale[z, h][:],
+                        rhs=x_code[z][:, lo:hi].bitcast(FP8X4),
+                        rhs_scale=x_scale[z][:, lo:hi],
                         start=(z == 0),
                         stop=(z == PASSES - 1),
                     )
         res = [keep.tile([P, S], F32, name=f"res{w}") for w in range(n_w)]
         for w in range(n_w):
-            for h in range(HALVES):
-                nc.scalar.copy(res[w][:, h * S_HALF : (h + 1) * S_HALF], acc[w, h][:])
+            for lo, hi in GROUPS[w]:
+                nc.scalar.copy(res[w][:, lo:hi], acc[w, lo][:])
         g, s, hh = res
 
         gc = keep.tile([P, V], F32, name="gc")

@@ -59,7 +59,7 @@ def tile_picked_filmg_relu_e_kernel(
 
         scale_words = w_scale[:].rearrange("p w z n -> p (w z n)").bitcast(I32)
         staged_words = staged[:].rearrange("p w z n -> p (w z n)").bitcast(I32)
-        nc.gpsimd.memset(scale_words, 0)
+        nc.vector.memset(scale_words, 0)
 
         for w in range(n_w):
             nc.scalar.dma_start(
@@ -70,7 +70,7 @@ def tile_picked_filmg_relu_e_kernel(
             if g == 0:
                 nc.sync.dma_start(offs_t[:], offs)
         for q in range(QUADS):
-            nc.gpsimd.dma_start(scale_words[32 * q : 32 * q + ROWS], staged_words[ROWS * q : ROWS * (q + 1)])
+            nc.scalar.dma_start(scale_words[32 * q : 32 * q + ROWS], staged_words[ROWS * q : ROWS * (q + 1)])
         for z in range(PASSES):
             for w in range(n_w):
                 nc.sync.dma_start(
@@ -126,7 +126,10 @@ def tile_picked_filmg_relu_e_kernel(
         res = [keep.tile([P, S], F32, name=f"res{w}") for w in range(n_w)]
         for w in range(n_w):
             for lo, hi in GROUPS[w]:
-                nc.scalar.copy(res[w][:, lo:hi], acc[w, lo][:])
+                if (w, lo) == (0, 0):
+                    nc.vector.tensor_copy(res[w][:, lo:hi], acc[w, lo][:])
+                else:
+                    nc.scalar.copy(res[w][:, lo:hi], acc[w, lo][:])
         g, s, hh = res
 
         gc = keep.tile([P, V], F32, name="gc")

@@ -13,14 +13,12 @@ U16 = mybir.dt.uint16
 U8 = mybir.dt.uint8
 FP8X4 = mybir.dt.float8_e4m3fn_x4
 ALU = mybir.AluOpType
-ACT = mybir.ActivationFunctionType
 
 P = 128
 PACK = 4
 K_PASS = P * PACK
 PASSES = K // K_PASS
 HALVES = 2
-S_HALF = S // HALVES
 LIST_COL = 16
 QUADS = 4
 ROWS = 4
@@ -83,28 +81,28 @@ def tile_picked_filmg_relu_e_kernel(
         x_code = {}
         x_scale = {}
         for z in range(PASSES):
-            picked = [keep.tile([P, S_HALF, PACK], BF16, name=f"picked{z}{h}", align_bytes=64) for h in range(HALVES)]
-            first = 0
-            if z == PASSES - 1:
-                first = 2
-                for h in range(HALVES):
-                    cols = slice(h * S_HALF // LIST_COL, (h + 1) * S_HALF // LIST_COL)
-                    pair = keep.tile([P, 2, S_HALF], F32, name=f"pair{h}")
-                    for j in range(first):
-                        nc.vector.tensor_copy(pair[:, j, :], plane[z, j].indirect(offs_t[:, cols]))
-                    nc.scalar.copy(picked[h][:, :, :first], pair[:].rearrange("p j s -> p s j"))
+            picked = keep.tile([P, S, PACK], BF16, name=f"picked{z}", align_bytes=64)
+            last = z == PASSES - 1
+            first = 2 if last else 0
+            if last:
+                pair = keep.tile([P, first, S], F32, name="pair")
+                for j in range(first):
+                    nc.vector.tensor_copy(pair[:, j, :], plane[z, j].indirect(offs_t[:]))
+                nc.scalar.copy(picked[:, :, :first], pair[:].rearrange("p j s -> p s j"))
             for j in range(first, PACK):
-                for h in range(HALVES):
-                    cols = slice(h * S_HALF // LIST_COL, (h + 1) * S_HALF // LIST_COL)
-                    nc.vector.tensor_copy(picked[h][:, :, j], plane[z, j].indirect(offs_t[:, cols]))
+                cuts = HALVES if last and j == PACK - 1 else 1
+                for c in range(cuts):
+                    lo, hi = c * S // cuts, (c + 1) * S // cuts
+                    nc.vector.tensor_copy(
+                        picked[:, lo:hi, j], plane[z, j].indirect(offs_t[:, lo // LIST_COL : hi // LIST_COL])
+                    )
             x_code[z] = keep.tile([P, S], U32, name=f"x_code{z}", align_bytes=64)
             x_scale[z] = keep.tile([P, S], U8, name=f"x_scale{z}", align_bytes=64)
             for lo, hi in GROUPS[0]:
-                h = lo // S_HALF
                 nc.vector.quantize_mx(
                     out=x_code[z][:, lo:hi].bitcast(FP8X4),
                     scales=x_scale[z][:, lo:hi],
-                    in_=picked[h][:, lo - h * S_HALF : hi - h * S_HALF].rearrange("p s j -> p (s j)"),
+                    in_=picked[:, lo:hi].rearrange("p s j -> p (s j)"),
                 )
 
         acc = {}
@@ -142,10 +140,14 @@ def tile_picked_filmg_relu_e_kernel(
         y = keep.tile([P, V], F32, name="y")
         nc.vector.tensor_copy(gc[:], g[:].indirect(cen_t[:]))
         nc.vector.tensor_copy(sc[:], s[:].indirect(cen_t[:]))
+        parts = [slice(i * V // 2, (i + 1) * V // 2) for i in range(2)]
         nc.vector.tensor_tensor(t1[:], hh[:].indirect(pos1_t[:]), gc[:], ALU.mult)
         nc.vector.tensor_tensor(t2[:], hh[:].indirect(pos2_t[:]), gc[:], ALU.mult)
-        nc.vector.tensor_tensor(a1[:], t1[:], sc[:], ALU.add)
-        nc.vector.tensor_tensor(a2[:], t2[:], sc[:], ALU.add)
-        nc.scalar.activation(r1[:], a1[:], ACT.Relu)
-        nc.vector.scalar_tensor_tensor(y[:], a2[:], 0.0, r1[:], ALU.max, ALU.add)
-        nc.sync.dma_start(out, y[:])
+        for part in parts:
+            nc.vector.tensor_tensor(a1[:, part], t1[:, part], sc[:, part], ALU.add)
+        for part in parts:
+            nc.vector.tensor_tensor(a2[:, part], t2[:, part], sc[:, part], ALU.add)
+            nc.vector.tensor_scalar(r1[:, part], a1[:, part], 0.0, None, ALU.max)
+        for part, queue in zip(parts, (nc.scalar, nc.sync)):
+            nc.vector.scalar_tensor_tensor(y[:, part], a2[:, part], 0.0, r1[:, part], ALU.max, ALU.add)
+            queue.dma_start(out[:, part], y[:, part])

@@ -13,16 +13,17 @@ U16 = mybir.dt.uint16
 U8 = mybir.dt.uint8
 FP8X4 = mybir.dt.float8_e4m3fn_x4
 ALU = mybir.AluOpType
+COPY = mybir.ActivationFunctionType.Copy
 
 P = 128
 PACK = 4
-K_PASS = P * PACK
-PASSES = K // K_PASS
-HALVES = 2
+PASSES = K // (P * PACK)
 LIST_COL = 16
 QUADS = 4
 ROWS = 4
-GROUPS = [[(0, 256), (256, 384), (384, 512)], [(0, 256), (256, 512)], [(0, 256), (256, 512)]]
+HALF = S // 2
+G, SH, H = 0, 1, 2
+SPANS = {G: [(0, 256), (256, 384), (384, 512)], H: [(0, 256), (256, 512)], SH: [(0, 256), (256, 512)]}
 
 
 def tile_picked_filmg_relu_e_kernel(
@@ -42,93 +43,76 @@ def tile_picked_filmg_relu_e_kernel(
         pos1_t = keep.tile([P, V // LIST_COL], U16, name="pos1_t")
         pos2_t = keep.tile([P, V // LIST_COL], U16, name="pos2_t")
 
-        groups = [(0, 0, 2), (0, 2, 2), (1, 0, 2), (1, 2, 1), (1, 3, 1)]
-        loaded = [keep.tile([P, n, T], F32, name=f"planes{z}{j}") for z, j, n in groups]
-        plane = {(z, j + i): loaded[g][:, i, :] for g, (z, j, n) in enumerate(groups) for i in range(n)}
+        loads = [(0, 0, 2), (0, 2, 2), (1, 0, 2), (1, 2, 1), (1, 3, 1)]
+        loaded = [keep.tile([P, n, T], F32, name=f"planes{z}{j}", align_bytes=64) for z, j, n in loads]
+        plane = {(z, j + i): loaded[u][:, i, :] for u, (z, j, n) in enumerate(loads) for i in range(n)}
         x_rows = xT.rearrange("(z p j) t -> z p j t", z=PASSES, j=PACK)
 
         staged = keep.tile([QUADS * ROWS, n_w, PASSES, N], U8, name="staged")
         w_scale = keep.tile([P, n_w, PASSES, N], U8, name="w_scale", align_bytes=64)
-        w_code = {
-            (w, z): keep.tile([P, N], U32, name=f"w_code{w}{z}", align_bytes=64)
-            for w in range(n_w)
-            for z in range(PASSES)
-        }
+        order = [(G, 0), (H, 0), (SH, 0), (G, 1), (H, 1), (SH, 1)]
+        w_code = {(w, z): keep.tile([P, N], U32, name=f"w_code{w}{z}", align_bytes=64) for w, z in order}
 
         scale_words = w_scale[:].rearrange("p w z n -> p (w z n)").bitcast(I32)
         staged_words = staged[:].rearrange("p w z n -> p (w z n)").bitcast(I32)
         nc.vector.memset(scale_words, 0)
 
         for w in range(n_w):
-            nc.scalar.dma_start(
-                staged[:, w].bitcast(I32), scales_in[w].rearrange("z s n -> s z n").bitcast(I32)
-            )
-        for g, (z, j, n) in enumerate(groups):
-            nc.sync.dma_start(loaded[g][:], x_rows[z, :, j : j + n, :])
-            if g == 0:
-                nc.sync.dma_start(offs_t[:], offs)
+            nc.scalar.dma_start(staged[:, w].bitcast(I32), scales_in[w].rearrange("z s n -> s z n").bitcast(I32))
+        nc.sync.dma_start(offs_t[:], offs)
+        for u, (z, j, n) in enumerate(loads):
+            nc.sync.dma_start(loaded[u][:], x_rows[z, :, j : j + n, :])
+            if u == 1:
+                nc.sync.dma_start(cen_t[:], cen)
         for q in range(QUADS):
             nc.scalar.dma_start(scale_words[32 * q : 32 * q + ROWS], staged_words[ROWS * q : ROWS * (q + 1)])
-        for z in range(PASSES):
-            for w in range(n_w):
-                nc.sync.dma_start(
-                    w_code[w, z][:].bitcast(I32), words_in[w][z].rearrange("p n t -> p (n t)").bitcast(I32)
-                )
-        nc.sync.dma_start(pos2_t[:], pos2)
+        for w, z in order:
+            nc.sync.dma_start(w_code[w, z][:].bitcast(I32), words_in[w][z].rearrange("p n t -> p (n t)").bitcast(I32))
         nc.sync.dma_start(pos1_t[:], pos1)
-        nc.sync.dma_start(cen_t[:], cen)
+        nc.sync.dma_start(pos2_t[:], pos2)
 
-        x_code = {}
-        x_scale = {}
+        picked = [keep.tile([P, S, PACK], BF16, name=f"picked{z}", align_bytes=64) for z in range(PASSES)]
+        for j in range(PACK):
+            nc.vector.tensor_copy(picked[0][:, :, j], plane[0, j].indirect(offs_t[:]))
+        pair = keep.tile([P, 2, S], F32, name="pair")
+        for j in range(2):
+            nc.vector.tensor_copy(pair[:, j, :], plane[1, j].indirect(offs_t[:]))
+        nc.scalar.copy(picked[1][:, :, :2], pair[:].rearrange("p j s -> p s j"))
+        nc.vector.tensor_copy(picked[1][:, :, 2], plane[1, 2].indirect(offs_t[:]))
+        row = keep.tile([P, HALF], BF16, name="row")
+        nc.vector.tensor_copy(picked[1][:, :HALF, 3], plane[1, 3].indirect(offs_t[:, : HALF // LIST_COL]))
+        nc.scalar.activation(row[:], plane[1, 3].indirect(offs_t[:, HALF // LIST_COL :]), COPY)
+        nc.vector.tensor_copy(picked[1][:, HALF:, 3], row[:])
+
+        x_code = [keep.tile([P, S], U32, name=tag, align_bytes=64) for tag in ("x_code0", "planes13")]
+        x_scale = [keep.tile([P, S], U8, name=f"x_scale{z}", align_bytes=64) for z in range(PASSES)]
         for z in range(PASSES):
-            picked = keep.tile([P, S, PACK], BF16, name=f"picked{z}", align_bytes=64)
-            last = z == PASSES - 1
-            first = 2 if last else 0
-            if last:
-                pair = keep.tile([P, first, S], F32, name="pair")
-                for j in range(first):
-                    nc.vector.tensor_copy(pair[:, j, :], plane[z, j].indirect(offs_t[:]))
-                nc.scalar.copy(picked[:, :, :first], pair[:].rearrange("p j s -> p s j"))
-            for j in range(first, PACK):
-                cuts = HALVES if last and j == PACK - 1 else 1
-                for c in range(cuts):
-                    lo, hi = c * S // cuts, (c + 1) * S // cuts
-                    nc.vector.tensor_copy(
-                        picked[:, lo:hi, j], plane[z, j].indirect(offs_t[:, lo // LIST_COL : hi // LIST_COL])
-                    )
-            x_code[z] = keep.tile([P, S], U32, name=f"x_code{z}", align_bytes=64)
-            x_scale[z] = keep.tile([P, S], U8, name=f"x_scale{z}", align_bytes=64)
-            for lo, hi in GROUPS[0]:
+            for lo, hi in SPANS[G]:
                 nc.vector.quantize_mx(
                     out=x_code[z][:, lo:hi].bitcast(FP8X4),
                     scales=x_scale[z][:, lo:hi],
-                    in_=picked[:, lo:hi].rearrange("p s j -> p (s j)"),
+                    in_=picked[z][:, lo:hi].rearrange("p s j -> p (s j)"),
                 )
 
-        acc = {}
-        for w in range(n_w):
-            for lo, hi in GROUPS[w]:
-                acc[w, lo] = psum.tile([P, hi - lo], F32, name=f"acc{w}_{lo}")
-        for z in range(PASSES):
-            for w in range(n_w):
-                for lo, hi in GROUPS[w]:
-                    nc.tensor.matmul_mx(
-                        out=acc[w, lo][:],
-                        lhsT=w_code[w, z][:].bitcast(FP8X4),
-                        lhsT_scale=w_scale[:, w, z, :],
-                        rhs=x_code[z][:, lo:hi].bitcast(FP8X4),
-                        rhs_scale=x_scale[z][:, lo:hi],
-                        start=(z == 0),
-                        stop=(z == PASSES - 1),
-                    )
-        res = [keep.tile([P, S], F32, name=f"res{w}") for w in range(n_w)]
-        for w in range(n_w):
-            for lo, hi in GROUPS[w]:
-                if (w, lo) == (0, 0):
-                    nc.vector.tensor_copy(res[w][:, lo:hi], acc[w, lo][:])
-                else:
-                    nc.scalar.copy(res[w][:, lo:hi], acc[w, lo][:])
-        g, s, hh = res
+        acc = {(w, lo): psum.tile([P, hi - lo], F32, name=f"acc{w}_{lo}") for w in SPANS for lo, hi in SPANS[w]}
+        for w, z in order:
+            for lo, hi in SPANS[w]:
+                nc.tensor.matmul_mx(
+                    out=acc[w, lo][:],
+                    lhsT=w_code[w, z][:].bitcast(FP8X4),
+                    lhsT_scale=w_scale[:, w, z, :],
+                    rhs=x_code[z][:, lo:hi].bitcast(FP8X4),
+                    rhs_scale=x_scale[z][:, lo:hi],
+                    start=(z == 0),
+                    stop=(z == PASSES - 1),
+                )
+        res = {w: keep.tile([P, S], F32, name=f"res{w}") for w in SPANS}
+
+        def drain(w, lo, hi, on_vector):
+            if on_vector:
+                nc.vector.tensor_copy(res[w][:, lo:hi], acc[w, lo][:])
+            else:
+                nc.scalar.copy(res[w][:, lo:hi], acc[w, lo][:])
 
         gc = keep.tile([P, V], F32, name="gc")
         sc = keep.tile([P, V], F32, name="sc")
@@ -138,11 +122,17 @@ def tile_picked_filmg_relu_e_kernel(
         a2 = keep.tile([P, V], F32, name="a2")
         r1 = keep.tile([P, V], F32, name="r1")
         y = keep.tile([P, V], F32, name="y")
-        nc.vector.tensor_copy(gc[:], g[:].indirect(cen_t[:]))
-        nc.vector.tensor_copy(sc[:], s[:].indirect(cen_t[:]))
+        for lo, hi in SPANS[G]:
+            drain(G, lo, hi, lo > 0)
+        nc.scalar.activation(gc[:], res[G][:].indirect(cen_t[:]), COPY)
+        for lo, hi in SPANS[H]:
+            drain(H, lo, hi, True)
+        for lo, hi in SPANS[SH]:
+            drain(SH, lo, hi, lo == 0)
+        nc.scalar.activation(sc[:], res[SH][:].indirect(cen_t[:]), COPY)
         parts = [slice(i * V // 2, (i + 1) * V // 2) for i in range(2)]
-        nc.vector.tensor_tensor(t1[:], hh[:].indirect(pos1_t[:]), gc[:], ALU.mult)
-        nc.vector.tensor_tensor(t2[:], hh[:].indirect(pos2_t[:]), gc[:], ALU.mult)
+        nc.vector.tensor_tensor(t1[:], res[H][:].indirect(pos1_t[:]), gc[:], ALU.mult)
+        nc.vector.tensor_tensor(t2[:], res[H][:].indirect(pos2_t[:]), gc[:], ALU.mult)
         for part in parts:
             nc.vector.tensor_tensor(a1[:, part], t1[:, part], sc[:, part], ALU.add)
         for part in parts:

@@ -50,8 +50,9 @@ def tile_picked_filmg_relu_e_kernel(
 
         staged = keep.tile([QUADS * ROWS, n_w, PASSES, N], U8, name="staged")
         w_scale = keep.tile([P, n_w, PASSES, N], U8, name="w_scale", align_bytes=64)
-        order = [(G, 0), (H, 0), (SH, 0), (G, 1), (H, 1), (SH, 1)]
-        w_code = {(w, z): keep.tile([P, N], U32, name=f"w_code{w}{z}", align_bytes=64) for w, z in order}
+        word_loads = [(w, z, 1) for z in range(PASSES) for w in (G, H, SH)]
+        word_tiles = [keep.tile([P, n, N], U32, name=f"w_code{w}{z}", align_bytes=64) for w, z, n in word_loads]
+        w_code = {(w, z + i): word_tiles[u][:, i, :] for u, (w, z, n) in enumerate(word_loads) for i in range(n)}
 
         scale_words = w_scale[:].rearrange("p w z n -> p (w z n)").bitcast(I32)
         staged_words = staged[:].rearrange("p w z n -> p (w z n)").bitcast(I32)
@@ -66,23 +67,26 @@ def tile_picked_filmg_relu_e_kernel(
                 nc.sync.dma_start(cen_t[:], cen)
         for q in range(QUADS):
             nc.scalar.dma_start(scale_words[32 * q : 32 * q + ROWS], staged_words[ROWS * q : ROWS * (q + 1)])
-        for w, z in order:
-            nc.sync.dma_start(w_code[w, z][:].bitcast(I32), words_in[w][z].rearrange("p n t -> p (n t)").bitcast(I32))
+        for u, (w, z, n) in enumerate(word_loads):
+            source = words_in[w][z : z + n].rearrange("z p n t -> p z (n t)")
+            nc.sync.dma_start(word_tiles[u][:].bitcast(I32), source.bitcast(I32))
         nc.sync.dma_start(pos1_t[:], pos1)
         nc.sync.dma_start(pos2_t[:], pos2)
 
         picked = [keep.tile([P, S, PACK], BF16, name=f"picked{z}", align_bytes=64) for z in range(PASSES)]
         for j in range(PACK):
             nc.vector.tensor_copy(picked[0][:, :, j], plane[0, j].indirect(offs_t[:]))
-        pair = keep.tile([P, 2, S], F32, name="pair")
-        for j in range(2):
-            nc.vector.tensor_copy(pair[:, j, :], plane[1, j].indirect(offs_t[:]))
-        nc.scalar.copy(picked[1][:, :, :2], pair[:].rearrange("p j s -> p s j"))
-        nc.vector.tensor_copy(picked[1][:, :, 2], plane[1, 2].indirect(offs_t[:]))
-        row = keep.tile([P, HALF], BF16, name="row")
-        nc.vector.tensor_copy(picked[1][:, :HALF, 3], plane[1, 3].indirect(offs_t[:, : HALF // LIST_COL]))
-        nc.scalar.activation(row[:], plane[1, 3].indirect(offs_t[:, HALF // LIST_COL :]), COPY)
-        nc.vector.tensor_copy(picked[1][:, HALF:, 3], row[:])
+        first, second = offs_t[:, : HALF // LIST_COL], offs_t[:, HALF // LIST_COL :]
+        rows = [keep.tile([P, 2, HALF], dtype, name=f"rows{u}") for u, dtype in enumerate((F32, BF16))]
+        for j in range(PACK):
+            nc.vector.tensor_copy(picked[1][:, :HALF, j], plane[1, j].indirect(first))
+            nc.scalar.activation(rows[j // 2][:, j % 2, :], plane[1, j].indirect(second), COPY)
+            if j == 1:
+                nc.vector.tensor_copy(picked[1][:, HALF:, :2], rows[0][:].rearrange("p j s -> p s j"))
+        quarter = HALF // 2
+        late = rows[1][:].rearrange("p j s -> p s j")
+        nc.vector.tensor_copy(picked[1][:, HALF : HALF + quarter, 2:], late[:, :quarter])
+        nc.scalar.copy(picked[1][:, HALF + quarter :, 2:], late[:, quarter:])
 
         x_code = [keep.tile([P, S], U32, name=tag, align_bytes=64) for tag in ("x_code0", "planes13")]
         x_scale = [keep.tile([P, S], U8, name=f"x_scale{z}", align_bytes=64) for z in range(PASSES)]
@@ -94,18 +98,25 @@ def tile_picked_filmg_relu_e_kernel(
                     in_=picked[z][:, lo:hi].rearrange("p s j -> p (s j)"),
                 )
 
-        acc = {(w, lo): psum.tile([P, hi - lo], F32, name=f"acc{w}_{lo}") for w in SPANS for lo, hi in SPANS[w]}
-        for w, z in order:
+        acc = {}
+
+        def product(w, z, lo, hi):
+            nc.tensor.matmul_mx(
+                out=acc[w, lo][:],
+                lhsT=w_code[w, z].bitcast(FP8X4),
+                lhsT_scale=w_scale[:, w, z, :],
+                rhs=x_code[z][:, lo:hi].bitcast(FP8X4),
+                rhs_scale=x_scale[z][:, lo:hi],
+                start=(z == 0),
+                stop=(z == PASSES - 1),
+            )
+
+        for w, z, n in word_loads:
             for lo, hi in SPANS[w]:
-                nc.tensor.matmul_mx(
-                    out=acc[w, lo][:],
-                    lhsT=w_code[w, z][:].bitcast(FP8X4),
-                    lhsT_scale=w_scale[:, w, z, :],
-                    rhs=x_code[z][:, lo:hi].bitcast(FP8X4),
-                    rhs_scale=x_scale[z][:, lo:hi],
-                    start=(z == 0),
-                    stop=(z == PASSES - 1),
-                )
+                if (w, lo) != (SH, HALF):
+                    if z == 0:
+                        acc[w, lo] = psum.tile([P, hi - lo], F32, name=f"acc{w}_{lo}")
+                    product(w, z, lo, hi)
         res = {w: keep.tile([P, S], F32, name=f"res{w}") for w in SPANS}
 
         def drain(w, lo, hi, on_vector):
@@ -124,6 +135,9 @@ def tile_picked_filmg_relu_e_kernel(
         y = keep.tile([P, V], F32, name="y")
         for lo, hi in SPANS[G]:
             drain(G, lo, hi, lo > 0)
+        acc[SH, HALF] = psum.tile([P, HALF], F32, name=f"acc{G}_0")
+        for z in range(PASSES):
+            product(SH, z, HALF, S)
         nc.scalar.activation(gc[:], res[G][:].indirect(cen_t[:]), COPY)
         for lo, hi in SPANS[H]:
             drain(H, lo, hi, True)

@@ -23,7 +23,7 @@ QUADS = 4
 ROWS = 4
 HALF = S // 2
 G, SH, H = 0, 1, 2
-SPANS = {G: [(0, 256), (256, 384), (384, 512)], H: [(0, 256), (256, 512)], SH: [(0, 256), (256, 512)]}
+SPANS = {G: [(0, 256), (256, 384), (384, 512)], H: [(0, 256), (256, 512)], SH: [(0, 256), (256, 384), (384, 512)]}
 
 
 def tile_picked_filmg_relu_e_kernel(
@@ -60,16 +60,17 @@ def tile_picked_filmg_relu_e_kernel(
 
         for w in range(n_w):
             nc.scalar.dma_start(staged[:, w].bitcast(I32), scales_in[w].rearrange("z s n -> s z n").bitcast(I32))
-        nc.sync.dma_start(offs_t[:], offs)
         for u, (z, j, n) in enumerate(loads):
             nc.sync.dma_start(loaded[u][:], x_rows[z, :, j : j + n, :])
-            if u == 1:
-                nc.sync.dma_start(cen_t[:], cen)
+            if u == 0:
+                nc.sync.dma_start(offs_t[:], offs)
         for q in range(QUADS):
             nc.scalar.dma_start(scale_words[32 * q : 32 * q + ROWS], staged_words[ROWS * q : ROWS * (q + 1)])
         for u, (w, z, n) in enumerate(word_loads):
             source = words_in[w][z : z + n].rearrange("z p n t -> p z (n t)")
             nc.sync.dma_start(word_tiles[u][:].bitcast(I32), source.bitcast(I32))
+            if u == 0:
+                nc.sync.dma_start(cen_t[:], cen)
         nc.sync.dma_start(pos1_t[:], pos1)
         nc.sync.dma_start(pos2_t[:], pos2)
 
@@ -113,7 +114,7 @@ def tile_picked_filmg_relu_e_kernel(
 
         for w, z, n in word_loads:
             for lo, hi in SPANS[w]:
-                if (w, lo) != (SH, HALF):
+                if w != SH or lo == 0:
                     if z == 0:
                         acc[w, lo] = psum.tile([P, hi - lo], F32, name=f"acc{w}_{lo}")
                     product(w, z, lo, hi)
@@ -135,9 +136,10 @@ def tile_picked_filmg_relu_e_kernel(
         y = keep.tile([P, V], F32, name="y")
         for lo, hi in SPANS[G]:
             drain(G, lo, hi, lo > 0)
-        acc[SH, HALF] = psum.tile([P, HALF], F32, name=f"acc{G}_0")
-        for z in range(PASSES):
-            product(SH, z, HALF, S)
+        for (lo, hi), (bank, end) in zip(SPANS[SH][1:], SPANS[G]):
+            acc[SH, lo] = psum.tile([P, hi - lo], F32, name=f"acc{G}_{bank}")
+            for z in range(PASSES):
+                product(SH, z, lo, hi)
         nc.scalar.activation(gc[:], res[G][:].indirect(cen_t[:]), COPY)
         for lo, hi in SPANS[H]:
             drain(H, lo, hi, True)

@@ -69,7 +69,7 @@ def tile_picked_filmg_relu_e_kernel(
         for u, (w, z, n) in enumerate(word_loads):
             source = words_in[w][z : z + n].rearrange("z p n t -> p z (n t)")
             nc.sync.dma_start(word_tiles[u][:].bitcast(I32), source.bitcast(I32))
-            if u == 0:
+            if (w, z) == (H, 1):
                 nc.sync.dma_start(cen_t[:], cen)
         nc.sync.dma_start(pos1_t[:], pos1)
         nc.sync.dma_start(pos2_t[:], pos2)
@@ -77,11 +77,13 @@ def tile_picked_filmg_relu_e_kernel(
         picked = [keep.tile([P, S, PACK], BF16, name=f"picked{z}", align_bytes=64) for z in range(PASSES)]
         for j in range(PACK):
             nc.vector.tensor_copy(picked[0][:, :, j], plane[0, j].indirect(offs_t[:]))
-        first, second = offs_t[:, : HALF // LIST_COL], offs_t[:, HALF // LIST_COL :]
+        first = offs_t[:, : HALF // LIST_COL]
         rows = [keep.tile([P, 2, HALF], dtype, name=f"rows{u}") for u, dtype in enumerate((F32, BF16))]
         for j in range(PACK):
             nc.vector.tensor_copy(picked[1][:, :HALF, j], plane[1, j].indirect(first))
-            nc.scalar.activation(rows[j // 2][:, j % 2, :], plane[1, j].indirect(second), COPY)
+            for lo, hi in SPANS[G][1:] if j == PACK - 1 else [(HALF, S)]:
+                window = plane[1, j].indirect(offs_t[:, lo // LIST_COL : hi // LIST_COL])
+                nc.scalar.activation(rows[j // 2][:, j % 2, lo - HALF : hi - HALF], window, COPY)
             if j == 1:
                 nc.vector.tensor_copy(picked[1][:, HALF:, :2], rows[0][:].rearrange("p j s -> p s j"))
         quarter = HALF // 2
@@ -145,8 +147,10 @@ def tile_picked_filmg_relu_e_kernel(
             drain(H, lo, hi, True)
         for lo, hi in SPANS[SH]:
             drain(SH, lo, hi, lo == 0)
-        nc.scalar.activation(sc[:], res[SH][:].indirect(cen_t[:]), COPY)
         parts = [slice(i * V // 2, (i + 1) * V // 2) for i in range(2)]
+        for part in parts:
+            columns = cen_t[:, part.start // LIST_COL : part.stop // LIST_COL]
+            nc.scalar.activation(sc[:, part], res[SH][:].indirect(columns), COPY)
         nc.vector.tensor_tensor(t1[:], res[H][:].indirect(pos1_t[:]), gc[:], ALU.mult)
         nc.vector.tensor_tensor(t2[:], res[H][:].indirect(pos2_t[:]), gc[:], ALU.mult)
         for part in parts:

@@ -22,6 +22,7 @@ LIST_COL = 16
 QUADS = 4
 ROWS = 4
 HALF = S // 2
+CUT = S - 64
 G, SH, H = 0, 1, 2
 SPANS = {G: [(0, 256), (256, 384), (384, 512)], H: [(0, 256), (256, 512)], SH: [(0, 256), (256, 384), (384, 512)]}
 
@@ -81,15 +82,14 @@ def tile_picked_filmg_relu_e_kernel(
         rows = [keep.tile([P, 2, HALF], dtype, name=f"rows{u}") for u, dtype in enumerate((F32, BF16))]
         for j in range(PACK):
             nc.vector.tensor_copy(picked[1][:, :HALF, j], plane[1, j].indirect(first))
-            for lo, hi in SPANS[G][1:] if j == PACK - 1 else [(HALF, S)]:
+            for lo, hi in [(HALF, CUT), (CUT, S)] if j == PACK - 1 else [(HALF, S)]:
                 window = plane[1, j].indirect(offs_t[:, lo // LIST_COL : hi // LIST_COL])
                 nc.scalar.activation(rows[j // 2][:, j % 2, lo - HALF : hi - HALF], window, COPY)
             if j == 1:
                 nc.vector.tensor_copy(picked[1][:, HALF:, :2], rows[0][:].rearrange("p j s -> p s j"))
-        quarter = HALF // 2
         late = rows[1][:].rearrange("p j s -> p s j")
-        nc.vector.tensor_copy(picked[1][:, HALF : HALF + quarter, 2:], late[:, :quarter])
-        nc.scalar.copy(picked[1][:, HALF + quarter :, 2:], late[:, quarter:])
+        nc.vector.tensor_copy(picked[1][:, HALF:CUT, 2:], late[:, : CUT - HALF])
+        nc.scalar.copy(picked[1][:, CUT:, 2:], late[:, CUT - HALF :])
 
         x_code = [keep.tile([P, S], U32, name=tag, align_bytes=64) for tag in ("x_code0", "planes13")]
         x_scale = [keep.tile([P, S], U8, name=f"x_scale{z}", align_bytes=64) for z in range(PASSES)]

@@ -22,9 +22,9 @@ LIST_COL = 16
 QUADS = 4
 ROWS = 4
 HALF = S // 2
-CUT = S - 64
+CUT = S - 128
 G, SH, H = 0, 1, 2
-SPANS = {G: [(0, 256), (256, 384), (384, 512)], H: [(0, 256), (256, 512)], SH: [(0, 256), (256, 384), (384, 512)]}
+SPANS = {G: [(0, 256), (256, 384), (384, 512)], H: [(0, 256), (256, 512)], SH: [(0, 128), (128, 256), (256, 384), (384, 512)]}
 
 
 def tile_picked_filmg_relu_e_kernel(
@@ -146,7 +146,7 @@ def tile_picked_filmg_relu_e_kernel(
         for lo, hi in SPANS[H]:
             drain(H, lo, hi, True)
         for lo, hi in SPANS[SH]:
-            drain(SH, lo, hi, lo == 0)
+            drain(SH, lo, hi, lo < HALF)
         parts = [slice(i * V // 2, (i + 1) * V // 2) for i in range(2)]
         for part in parts:
             columns = cen_t[:, part.start // LIST_COL : part.stop // LIST_COL]

@@ -45,7 +45,7 @@ def tile_picked_filmg_relu_e_kernel(
         pos2_t = keep.tile([P, V // LIST_COL], U16, name="pos2_t")
 
         loads = [(0, 0, 2), (0, 2, 2), (1, 0, 2), (1, 2, 1), (1, 3, 1)]
-        loaded = [keep.tile([P, n, T], F32, name=f"planes{z}{j}", align_bytes=64) for z, j, n in loads]
+        loaded = [keep.tile([P, n, T], F32, name=f"planes{z}{j}", align_bytes=256) for z, j, n in loads]
         plane = {(z, j + i): loaded[u][:, i, :] for u, (z, j, n) in enumerate(loads) for i in range(n)}
         x_rows = xT.rearrange("(z p j) t -> z p j t", z=PASSES, j=PACK)
 
@@ -91,7 +91,7 @@ def tile_picked_filmg_relu_e_kernel(
         nc.vector.tensor_copy(picked[1][:, HALF:CUT, 2:], late[:, : CUT - HALF])
         nc.scalar.copy(picked[1][:, CUT:, 2:], late[:, CUT - HALF :])
 
-        x_code = [keep.tile([P, S], U32, name=tag, align_bytes=64) for tag in ("x_code0", "planes13")]
+        x_code = [keep.tile([P, S], U32, name=tag, align_bytes=256) for tag in ("x_code0", "planes13")]
         x_scale = [keep.tile([P, S], U8, name=f"x_scale{z}", align_bytes=64) for z in range(PASSES)]
         for z in range(PASSES):
             for lo, hi in SPANS[G]:

@@ -49,10 +49,10 @@ def tile_picked_filmg_relu_e_kernel(
         plane = {(z, j + i): loaded[u][:, i, :] for u, (z, j, n) in enumerate(loads) for i in range(n)}
         x_rows = xT.rearrange("(z p j) t -> z p j t", z=PASSES, j=PACK)
 
-        staged = keep.tile([QUADS * ROWS, n_w, PASSES, N], U8, name="staged")
-        w_scale = keep.tile([P, n_w, PASSES, N], U8, name="w_scale", align_bytes=64)
+        staged = keep.tile([QUADS * ROWS, n_w, PASSES, N], U8, name="staged", align_bytes=256)
+        w_scale = keep.tile([P, n_w, PASSES, N], U8, name="w_scale", align_bytes=256)
         word_loads = [(w, z, 1) for z in range(PASSES) for w in (G, H, SH)]
-        word_tiles = [keep.tile([P, n, N], U32, name=f"w_code{w}{z}", align_bytes=64) for w, z, n in word_loads]
+        word_tiles = [keep.tile([P, n, N], U32, name=f"w_code{w}{z}", align_bytes=256) for w, z, n in word_loads]
         w_code = {(w, z + i): word_tiles[u][:, i, :] for u, (w, z, n) in enumerate(word_loads) for i in range(n)}
 
         scale_words = w_scale[:].rearrange("p w z n -> p (w z n)").bitcast(I32)
@@ -135,7 +135,7 @@ def tile_picked_filmg_relu_e_kernel(
         a1 = keep.tile([P, V], F32, name="a1")
         a2 = keep.tile([P, V], F32, name="a2")
         r1 = keep.tile([P, V], F32, name="r1")
-        y = keep.tile([P, V], F32, name="y")
+        y = keep.tile([P, V], F32, name="y", align_bytes=256)
         for lo, hi in SPANS[G]:
             drain(G, lo, hi, lo > 0)
         for (lo, hi), (bank, end) in zip(SPANS[SH][1:], SPANS[G]):

from contextlib import ExitStack

import concourse.mybir as mybir

K, T, S, V, N = 1024, 2048, 512, 256, 128
FLOPS = 3 * 2 * K * S * N

F32 = mybir.dt.float32
BF16 = mybir.dt.bfloat16
I32 = mybir.dt.int32
U32 = mybir.dt.uint32
U16 = mybir.dt.uint16
U8 = mybir.dt.uint8
FP8X4 = mybir.dt.float8_e4m3fn_x4
ALU = mybir.AluOpType
COPY = mybir.ActivationFunctionType.Copy

P = 128
PACK = 4
PASSES = K // (P * PACK)
LIST_COL = 16
QUADS = 4
ROWS = 4
HALF = S // 2
CUT = S - 128
G, SH, H = 0, 1, 2
SPANS = {G: [(0, 256), (256, 384), (384, 512)], H: [(0, 256), (256, 512)], SH: [(0, 128), (128, 256), (256, 384), (384, 512)]}


def tile_picked_filmg_relu_e_kernel(
    tc, xT, w1_words, w1_scales, w2_words, w2_scales, w3_words, w3_scales, offs, cen, pos1, pos2, out
):
    nc = tc.nc
    words_in = [w1_words, w2_words, w3_words]
    scales_in = [w1_scales, w2_scales, w3_scales]
    n_w = len(words_in)

    with ExitStack() as ctx:
        keep = ctx.enter_context(tc.tile_pool(name="keep", bufs=1))
        psum = ctx.enter_context(tc.psum_pool(name="psum", bufs=1))

        offs_t = keep.tile([P, S // LIST_COL], U16, name="offs_t")
        cen_t = keep.tile([P, V // LIST_COL], U16, name="cen_t")
        pos1_t = keep.tile([P, V // LIST_COL], U16, name="pos1_t")
        pos2_t = keep.tile([P, V // LIST_COL], U16, name="pos2_t")

        loads = [(0, 0, 2), (0, 2, 2), (1, 0, 2), (1, 2, 1), (1, 3, 1)]
        loaded = [keep.tile([P, n, T], F32, name=f"planes{z}{j}", align_bytes=256) for z, j, n in loads]
        plane = {(z, j + i): loaded[u][:, i, :] for u, (z, j, n) in enumerate(loads) for i in range(n)}
        x_rows = xT.rearrange("(z p j) t -> z p j t", z=PASSES, j=PACK)

        staged = keep.tile([QUADS * ROWS, n_w, PASSES, N], U8, name="staged", align_bytes=256)
        w_scale = keep.tile([P, n_w, PASSES, N], U8, name="w_scale", align_bytes=256)
        word_loads = [(w, z, 1) for z in range(PASSES) for w in (G, H, SH)]
        word_tiles = [keep.tile([P, n, N], U32, name=f"w_code{w}{z}", align_bytes=256) for w, z, n in word_loads]
        w_code = {(w, z + i): word_tiles[u][:, i, :] for u, (w, z, n) in enumerate(word_loads) for i in range(n)}

        scale_words = w_scale[:].rearrange("p w z n -> p (w z n)").bitcast(I32)
        staged_words = staged[:].rearrange("p w z n -> p (w z n)").bitcast(I32)
        nc.vector.memset(scale_words, 0)

        for w in range(n_w):
            nc.scalar.dma_start(staged[:, w].bitcast(I32), scales_in[w].rearrange("z s n -> s z n").bitcast(I32))
        for u, (z, j, n) in enumerate(loads):
            nc.sync.dma_start(loaded[u][:], x_rows[z, :, j : j + n, :])
            if u == 0:
                nc.sync.dma_start(offs_t[:], offs)
        for q in range(QUADS):
            nc.scalar.dma_start(scale_words[32 * q : 32 * q + ROWS], staged_words[ROWS * q : ROWS * (q + 1)])
        for u, (w, z, n) in enumerate(word_loads):
            source = words_in[w][z : z + n].rearrange("z p n t -> p z (n t)")
            nc.sync.dma_start(word_tiles[u][:].bitcast(I32), source.bitcast(I32))
            if (w, z) == (H, 1):
                nc.sync.dma_start(cen_t[:], cen)
        nc.sync.dma_start(pos1_t[:], pos1)
        nc.sync.dma_start(pos2_t[:], pos2)

        picked = [keep.tile([P, S, PACK], BF16, name=f"picked{z}", align_bytes=64) for z in range(PASSES)]
        for j in range(PACK):
            nc.vector.tensor_copy(picked[0][:, :, j], plane[0, j].indirect(offs_t[:]))
        first = offs_t[:, : HALF // LIST_COL]
        rows = [keep.tile([P, 2, HALF], dtype, name=f"rows{u}") for u, dtype in enumerate((F32, BF16))]
        for j in range(PACK):
            nc.vector.tensor_copy(picked[1][:, :HALF, j], plane[1, j].indirect(first))
            for lo, hi in [(HALF, CUT), (CUT, S)] if j == PACK - 1 else [(HALF, S)]:
                window = plane[1, j].indirect(offs_t[:, lo // LIST_COL : hi // LIST_COL])
                nc.scalar.activation(rows[j // 2][:, j % 2, lo - HALF : hi - HALF], window, COPY)
            if j == 1:
                nc.vector.tensor_copy(picked[1][:, HALF:, :2], rows[0][:].rearrange("p j s -> p s j"))
        late = rows[1][:].rearrange("p j s -> p s j")
        nc.vector.tensor_copy(picked[1][:, HALF:CUT, 2:], late[:, : CUT - HALF])
        nc.scalar.copy(picked[1][:, CUT:, 2:], late[:, CUT - HALF :])

        x_code = [keep.tile([P, S], U32, name=tag, align_bytes=256) for tag in ("x_code0", "planes13")]
        x_scale = [keep.tile([P, S], U8, name=f"x_scale{z}", align_bytes=64) for z in range(PASSES)]
        for z in range(PASSES):
            for lo, hi in SPANS[G]:
                nc.vector.quantize_mx(
                    out=x_code[z][:, lo:hi].bitcast(FP8X4),
                    scales=x_scale[z][:, lo:hi],
                    in_=picked[z][:, lo:hi].rearrange("p s j -> p (s j)"),
                )

        acc = {}

        def product(w, z, lo, hi):
            nc.tensor.matmul_mx(
                out=acc[w, lo][:],
                lhsT=w_code[w, z].bitcast(FP8X4),
                lhsT_scale=w_scale[:, w, z, :],
                rhs=x_code[z][:, lo:hi].bitcast(FP8X4),
                rhs_scale=x_scale[z][:, lo:hi],
                start=(z == 0),
                stop=(z == PASSES - 1),
            )

        for w, z, n in word_loads:
            for lo, hi in SPANS[w]:
                if w != SH or lo == 0:
                    if z == 0:
                        acc[w, lo] = psum.tile([P, hi - lo], F32, name=f"acc{w}_{lo}")
                    product(w, z, lo, hi)
        res = {w: keep.tile([P, S], F32, name=f"res{w}") for w in SPANS}

        def drain(w, lo, hi, on_vector):
            if on_vector:
                nc.vector.tensor_copy(res[w][:, lo:hi], acc[w, lo][:])
            else:
                nc.scalar.copy(res[w][:, lo:hi], acc[w, lo][:])

        gc = keep.tile([P, V], F32, name="gc")
        sc = keep.tile([P, V], F32, name="sc")
        t1 = keep.tile([P, V], F32, name="t1")
        t2 = keep.tile([P, V], F32, name="t2")
        a1 = keep.tile([P, V], F32, name="a1")
        a2 = keep.tile([P, V], F32, name="a2")
        r1 = keep.tile([P, V], F32, name="r1")
        y = keep.tile([P, V], F32, name="y", align_bytes=256)
        for lo, hi in SPANS[G]:
            drain(G, lo, hi, lo > 0)
        for (lo, hi), (bank, end) in zip(SPANS[SH][1:], SPANS[G]):
            acc[SH, lo] = psum.tile([P, hi - lo], F32, name=f"acc{G}_{bank}")
            for z in range(PASSES):
                product(SH, z, lo, hi)
        nc.scalar.activation(gc[:], res[G][:].indirect(cen_t[:]), COPY)
        for lo, hi in SPANS[H]:
            drain(H, lo, hi, True)
        for lo, hi in SPANS[SH]:
            drain(SH, lo, hi, lo < HALF)
        parts = [slice(i * V // 2, (i + 1) * V // 2) for i in range(2)]
        for part in parts:
            columns = cen_t[:, part.start // LIST_COL : part.stop // LIST_COL]
            nc.scalar.activation(sc[:, part], res[SH][:].indirect(columns), COPY)
        nc.vector.tensor_tensor(t1[:], res[H][:].indirect(pos1_t[:]), gc[:], ALU.mult)
        nc.vector.tensor_tensor(t2[:], res[H][:].indirect(pos2_t[:]), gc[:], ALU.mult)
        for part in parts:
            nc.vector.tensor_tensor(a1[:, part], t1[:, part], sc[:, part], ALU.add)
        for part in parts:
            nc.vector.tensor_tensor(a2[:, part], t2[:, part], sc[:, part], ALU.add)
            nc.vector.tensor_scalar(r1[:, part], a1[:, part], 0.0, None, ALU.max)
        for part, queue in zip(parts, (nc.scalar, nc.sync)):
            nc.vector.scalar_tensor_tensor(y[:, part], a2[:, part], 0.0, r1[:, part], ALU.max, ALU.add)
            queue.dma_start(out[:, part], y[:, part])
